import numpy as np
import ml_dtypes


def mxq(x, axis, fmt="e4m3"):
    dtype, down = {"e4m3": (ml_dtypes.float8_e4m3fn, 7), "e5m2": (ml_dtypes.float8_e5m2, 14)}[fmt]
    v = np.moveaxis(np.asarray(x, np.float32).astype(ml_dtypes.bfloat16).astype(np.float64), axis, -1)
    blocks = v.reshape(v.shape[:-1] + (-1, 32))
    amax = np.abs(blocks).max(-1, keepdims=True)
    byte = np.maximum(np.where(amax > 0, np.frexp(amax)[1] - 1 + 127, 0) - down, 1)
    scale = np.exp2(byte - 127.0)
    codes = (blocks / scale).astype(np.float32).astype(dtype).astype(np.float64)
    return np.moveaxis((codes * scale).reshape(v.shape), -1, axis)


WIDE = False


def mx_kscale(k):
    if not WIDE:
        return np.ones(k)
    levels = np.array([10, -10, 5, -5, 0])
    if k % 512:
        return np.exp2(np.random.permutation(np.resize(levels, k // 32))).repeat(32)
    a = np.empty((k // 512, 16))
    for p in range(k // 512):
        a[p, :8] = np.random.permutation(np.resize(levels, 8))
        for g in range(8):
            far = levels[np.abs(levels - a[p, g]) >= 10]
            a[p, g + 8] = far[np.random.randint(len(far))]
    return np.exp2(a.ravel()).repeat(32)


def f64(x):
    return np.asarray(x).astype(np.float64)


def striped(idx):
    return np.tile(idx.reshape(-1, 16).T, (8, 1)).astype(np.uint16)


def unstriped(offs):
    return offs[:16].T.reshape(-1).astype(np.int64)


E2M1 = np.array([0.0, 0.5, 1.0, 1.5, 2.0, 3.0, 4.0, 6.0, -0.0, -0.5, -1.0, -1.5, -2.0, -3.0, -4.0, -6.0])


def pack_weight(w, fmt):
    k, n = w.shape
    w = f64(np.asarray(w, np.float32).astype(ml_dtypes.bfloat16)).reshape(k // 32, 32, n)
    amax = np.abs(w).max(1)
    if fmt == "e4m3":
        byte = np.frexp(amax)[1] - 1 + 127 - 7
    else:
        mant, ex = np.frexp(amax / 6.0)
        byte = np.where(mant > 0.5, ex, ex - 1) + 127
    byte = np.clip(np.where(amax > 0, byte, 1), 1, 254)
    scaled = (w * np.exp2(127.0 - byte)[:, None, :]).reshape(k, n).astype(np.float32)
    by_word = np.ascontiguousarray(scaled.reshape(k // 512, 128, 4, n).transpose(0, 1, 3, 2))
    if fmt == "e4m3":
        words = by_word.astype(ml_dtypes.float8_e4m3fn).view(np.uint8)
    else:
        c = by_word.astype(ml_dtypes.float4_e2m1fn).view(np.uint8) & 0xF
        words = (c[..., 0::2] | (c[..., 1::2] << 4)).reshape(k // 512, 128, 2 * n)
    return np.ascontiguousarray(words), np.ascontiguousarray(byte.astype(np.uint8).reshape(k // 512, 16, n))


def unpack_weight(words, scales, fmt):
    g, _, n = scales.shape
    words = np.ascontiguousarray(words).reshape(g, 128, n, -1)
    if fmt == "e4m3":
        vals = words.view(ml_dtypes.float8_e4m3fn).astype(np.float64)
    else:
        nib = np.empty((g, 128, n, 4), np.uint8)
        nib[..., 0::2] = words & 0xF
        nib[..., 1::2] = words >> 4
        vals = E2M1[nib]
    vals = vals * np.repeat(np.exp2(scales.astype(np.float64) - 127.0), 8, axis=1)[..., None]
    return vals.transpose(0, 1, 3, 2).reshape(g * 512, n)


def gelu(v):
    return 0.5 * v * (1.0 + np.tanh(np.sqrt(2.0 / np.pi) * (v + 0.044715 * v**3)))


K, T, S, H, T2, P, N = 1536, 2048, 512, 1024, 2048, 1024, 768

def setup_inputs():
    n = np.random.standard_normal
    s = mx_kscale(K)[:, None]
    u = mx_kscale(H)[:, None]
    d = {}
    d["tab_words"], d["tab_scales"] = pack_weight(n((K, T)) * s, "e4m3")
    d["tab2_words"], d["tab2_scales"] = pack_weight(n((K, T)) * s, "e4m3")
    d["offs"] = striped(np.random.permutation(T)[:S])
    d["offs2"] = striped(np.random.permutation(T)[:S])
    perm = np.random.permutation(T2)
    d["offs3"] = striped(perm[:S])
    d["offs4"] = striped(perm[S:2 * S])
    d["offs5"] = striped(np.random.permutation(T2)[:P])
    d["w1"] = (1.5 * n((K, H)) / K ** 0.5 / s).astype(np.float32)
    d["gf"] = (1.3 * np.exp(0.3 * n(H)) * u[:, 0]).astype(np.float32)
    d["gb"] = (0.4 * np.exp(0.3 * n(H)) * u[:, 0]).astype(np.float32)
    d["wg1"] = np.exp(0.3 * n((128, S))).astype(np.float32)
    d["wg2"] = np.exp(0.3 * n((128, S))).astype(np.float32)
    d["page0"] = (n((H, T2)) * u).astype(np.float32)
    d["lvl"] = ((0.3 + 0.6 * n(H)) * u[:, 0]).astype(np.float32)
    d["w4_words"], d["w4_scales"] = pack_weight(n((H, N)) / H ** 0.5 / u, "e2m1")
    d["gain"] = np.exp(0.3 * n(N)).astype(np.float32)
    return d

def reference(tab_words, tab_scales, tab2_words, tab2_scales, offs, offs2, offs3, offs4, offs5, w1, gf, gb, wg1, wg2, page0, lvl, w4_words, w4_scales, gain):
    v = unpack_weight(tab_words, tab_scales, "e4m3")[:, unstriped(offs)]
    v2 = unpack_weight(tab2_words, tab2_scales, "e4m3")[:, unstriped(offs2)]
    w1q = mxq(f64(w1), 0, "e4m3")
    h1 = f64(gf)[:, None] * np.tanh(w1q.T @ v)
    h2 = f64(gb)[:, None] * np.square(w1q.T @ v2)
    page = f64(page0).copy()
    page[:, unstriped(offs3)] = np.tile(f64(wg1), (H // 128, 1)) * h1
    page[:, unstriped(offs4)] = np.tile(f64(wg2), (H // 128, 1)) * h2
    x = page[:, unstriped(offs5)] - f64(lvl)[:, None]
    xq = mxq(x, 0, "e4m3")
    w4 = unpack_weight(w4_words, w4_scales, "e2m1")
    y = w4.T @ xq
    return f64(gain)[:, None] * y

@@ -1,0 +1,282 @@
+from contextlib import ExitStack
+
+import concourse.mybir as mybir
+
+K, T, S, H, T2, PICK, N = 1536, 2048, 512, 1024, 2048, 1024, 768
+FLOPS = 2 * (2 * K * H * S + H * N * PICK)
+
+F32 = mybir.dt.float32
+BF16 = mybir.dt.bfloat16
+I32 = mybir.dt.int32
+U32 = mybir.dt.uint32
+U16 = mybir.dt.uint16
+U8 = mybir.dt.uint8
+FP8X4 = mybir.dt.float8_e4m3fn_x4
+FP4X4 = mybir.dt.float4_e2m1fn_x4
+ACT = mybir.ActivationFunctionType
+ALU = mybir.AluOpType
+
+P = 128
+PACK = 4
+PASS = P * PACK
+KP = K // PASS
+HB = H // PASS
+NT = N // P
+HALF = 512
+RING = 6
+QUARTER = 256
+BANKS = 8
+ON_VECTOR = (0, 1, 2, 4, 6, 8, 10)
+
+
+def tile_list_banknote_fitness_archive_kernel(
+    tc, tab_words, tab_scales, tab2_words, tab2_scales, offs, offs2, offs3, offs4, offs5,
+    w1, gf, gb, wg1, wg2, page0, lvl, w4_words, w4_scales, gain, out,
+):
+    nc = tc.nc
+    with ExitStack() as ctx:
+        sb = ctx.enter_context(tc.tile_pool(name="sb", bufs=1))
+        ps = ctx.enter_context(tc.psum_pool(name="ps", bufs=1))
+
+        def tile(shape, dtype, name, tag=None):
+            return sb.tile(shape, dtype, name=name, tag=tag or name, align_bytes=64)
+
+        lists = {}
+
+        def load_list(name, ap):
+            lists[name] = tile([P, ap.shape[1]], U16, "list_" + name)
+            nc.sync.dma_start(lists[name][:], ap)
+
+        banks = [ps.tile([P, HALF], F32, name="bank%d" % i, tag="bank%d" % i) for i in range(BANKS)]
+        raw = [tile([P, PACK * PASS], F32, "raw%d" % a) for a in range(KP)]
+        grouped = [tile([P, PACK * PASS], BF16, "grouped%d" % i) for i in range(KP)]
+        w1_codes = [[tile([P, PASS], U32, "w1c%d%d" % (b, a)) for a in range(KP)] for b in range(HB)]
+        w1_scales = [[tile([P, PASS], U8, "w1s%d%d" % (b, a)) for a in range(KP)] for b in range(HB)]
+        words = [[tile([P, T], U32, "words%d%d" % (s, a)) for a in range(KP)] for s in range(2)]
+        scale_win = [tile([P, T], U8, "scalewin%d" % s) for s in range(2)]
+        v_codes = [[tile([P, S], U32, "vc%d%d" % (s, a)) for a in range(KP)] for s in range(2)]
+        v_scales = [tile([P, S], U8, "vs%d" % s) for s in range(2)]
+        pages = [tile([P, T2], F32, "page%d" % u) for u in range(HB * PACK)]
+        wg1_sb = [tile([P, S], F32, "wg1_%d" % t) for t in range(PACK)]
+        wg2_first = tile([P, S], F32, "wg2_first")
+        wg2_rest = tile([P, (PACK - 1) * S], F32, "wg2_rest")
+        dealt = [[wg1_sb[t][:] for t in range(PACK)],
+                 [wg2_first[:]] + [wg2_rest[:, t * S:(t + 1) * S] for t in range(PACK - 1)]]
+        first = [[tile([P, S], F32, "factor%d%d" % (s, t)) for t in range(PACK)] for s in range(2)]
+        factor = [[first[s][t][:] for t in range(PACK)] + dealt[s] for s in range(2)]
+        feat = [tile([P, S], F32, "feat%d" % i) for i in range(RING)]
+        w4c = tile([P, HB, 2 * N], U8, "w4c")
+        w4s = tile([P, HB, N], U8, "w4s")
+        rowgain = [tile([P, HB, PACK], F32, "rowgain%d" % s) for s in range(2)]
+        lvl_sb = tile([P, HB, PACK], F32, "lvl_sb")
+        neg_lvl = tile([P, HB, PACK], F32, "neg_lvl")
+        gain_sb = tile([P, NT], F32, "gain_sb")
+        zero_in = tile([P, 1], F32, "zero_in")
+        zero = tile([P, 1], F32, "zero")
+        x_codes = [tile([P, PICK], U32, "xc%d" % b, tag="words1%d" % b) for b in range(HB)]
+        x_scales = [tile([P, PICK], U8, "xs%d" % b) for b in range(HB)]
+
+        def load_w1(b, a):
+            nc.sync.dma_start(
+                raw[a][:].rearrange("p (j c) -> p j c", j=PACK),
+                w1[a * PASS:(a + 1) * PASS, b * PASS:(b + 1) * PASS].rearrange("(p j) c -> p j c", j=PACK))
+
+        def load_words(s, a):
+            src = (tab_words, tab2_words)[s]
+            nc.sync.dma_start(words[s][a][:].bitcast(I32), src[a].rearrange("p t i -> p (t i)").bitcast(I32))
+
+        def load_scales(eng, s):
+            src = (tab_scales, tab2_scales)[s]
+            for q in range(4):
+                eng.dma_start(scale_win[s][32 * q:32 * q + 4 * KP, :].bitcast(I32),
+                                    src[:, 4 * q:4 * q + 4, :].bitcast(I32))
+
+        def load_page(u):
+            b, t = divmod(u, PACK)
+            nc.sync.dma_start(pages[u][:], page0.rearrange("(b p t) c -> b t p c", b=HB, t=PACK)[b, t])
+
+        def load_dealt(eng, dst, src, t0, t1):
+            rows = src.rearrange("(q t) j -> q (t j)", t=PACK)[:, t0 * S:t1 * S]
+            for q in range(4):
+                eng.dma_start(dst[32 * q:32 * q + 32, :], rows)
+
+        def load_rowvec(eng, dst, src):
+            eng.dma_start(dst[:], src.rearrange("(b p t) -> p b t", b=HB, t=PACK))
+
+        def quantize_w1(b, a):
+            g = grouped[a]
+            nc.scalar.copy(g[:].rearrange("p (t m j) -> p m j t", t=PACK, j=PACK),
+                           raw[a][:].rearrange("p (j m t) -> p m j t", j=PACK, t=PACK))
+            nc.vector.quantize_mx(out=w1_codes[b][a][:].bitcast(FP8X4), scales=w1_scales[b][a][:], in_=g[:])
+
+        def gather_table(s):
+            lst = lists[("offs", "offs2")[s]]
+            nc.vector.tensor_copy(v_scales[s][:], scale_win[s][:].indirect(lst[:]))
+            for a in range(KP):
+                nc.vector.tensor_copy(v_codes[s][a][:], words[s][a][:].indirect(lst[:]))
+
+        puts = []
+
+        def put(s, u):
+            n = len(puts)
+            puts.append((s, u))
+            b, t = divmod(u, PACK)
+            bank = banks[n % BANKS]
+            cols = slice(t * P, (t + 1) * P)
+            for a in range(KP):
+                nc.tensor.matmul_mx(
+                    out=bank[:], lhsT=w1_codes[b][a][:, cols].bitcast(FP8X4), lhsT_scale=w1_scales[b][a][:, cols],
+                    rhs=v_codes[s][a][:].bitcast(FP8X4), rhs_scale=v_scales[s][4 * a:P, :],
+                    start=(a == 0), stop=(a == KP - 1))
+            nc.scalar.activation(factor[s][u], dealt[s][t], ACT.Copy, scale=rowgain[s][:, b, t:t + 1])
+            nc.scalar.activation(feat[n % RING][:], bank[:], (ACT.Tanh, ACT.Square)[s], bias=zero[:])
+            lst = lists[("offs3", "offs4")[s]]
+            nc.vector.tensor_tensor(pages[u][:].indirect(lst[:]), feat[n % RING][:], factor[s][u], ALU.mult)
+
+        woven = {}
+
+        def fetch(u, m0=0, m1=PICK, at=None):
+            at = m0 if at is None else at
+            nc.vector.tensor_copy(raw[u % KP][:, at:at + m1 - m0], pages[u][:].indirect(lists["offs5"][:, m0 // 16:m1 // 16]))
+
+        def level(u, m0=0, m1=PICK, at=None):
+            at = m0 if at is None else at
+            b, t = divmod(u, PACK)
+            if b not in woven:
+                woven[b] = tile([P, PICK * PACK], BF16, "woven%d" % b, tag="words0%d" % b)
+            nc.scalar.activation(
+                woven[b][:].rearrange("p (m t) -> p m t", t=PACK)[:, m0:m1, t],
+                raw[u % KP][:, at:at + m1 - m0], ACT.Identity, bias=neg_lvl[:, b, t:t + 1])
+
+        def quantize_x(b, m0=0, m1=PICK):
+            nc.vector.quantize_mx(out=x_codes[b][:, m0:m1].bitcast(FP8X4), scales=x_scales[b][:, m0:m1],
+                                  in_=woven[b][:, PACK * m0:PACK * m1])
+
+        def score(bank, b, unit):
+            m0, width, ns = unit
+            step = HALF if width == HALF else P
+            passes = [(i, n, c) for i, n in enumerate(ns) for c in range(0, width, step)]
+            for k, (i, n, c) in enumerate(passes):
+                nc.tensor.matmul_mx(
+                    out=bank[:, i * width + c:i * width + c + step],
+                    lhsT=w4c[:, b, 2 * P * n:2 * P * (n + 1)].bitcast(FP4X4),
+                    lhsT_scale=w4s[:, b, P * n:P * (n + 1)],
+                    rhs=x_codes[b][:, m0 + c:m0 + c + step].bitcast(FP8X4),
+                    rhs_scale=x_scales[b][:, m0 + c:m0 + c + step],
+                    start=(b == 0 and k == 0), stop=(b == HB - 1 and k == len(passes) - 1))
+
+        nc.vector.memset(zero_in[:], 0.0)
+        nc.scalar.activation(zero[:], zero_in[:], ACT.Tanh)
+        for s in range(2):
+            nc.vector.memset(scale_win[s][:].bitcast(I32), 0)
+        nc.vector.memset(w4s[:].rearrange("p b n -> p (b n)").bitcast(I32), 0)
+
+        load_scales(nc.gpsimd, 0)
+        load_rowvec(nc.gpsimd, rowgain[0], gf)
+        load_scales(nc.gpsimd, 1)
+        load_rowvec(nc.gpsimd, rowgain[1], gb)
+        for q in range(4):
+            nc.gpsimd.dma_start(w4s[32 * q:32 * q + 4, :, :].bitcast(I32),
+                                w4_scales[:, 4 * q:4 * q + 4, :].rearrange("b r n -> r b n").bitcast(I32))
+
+        load_w1(0, 0)
+        load_list("offs", offs)
+        load_w1(0, 1)
+        load_list("offs3", offs3)
+        load_w1(0, 2)
+        load_list("offs2", offs2)
+        load_words(0, 0)
+        load_words(0, 1)
+        load_words(0, 2)
+        load_dealt(nc.sync, wg1_sb[0], wg1, 0, 1)
+        load_page(0)
+        for t in (1, 2):
+            load_dealt(nc.sync, wg1_sb[t], wg1, t, t + 1)
+            load_page(t)
+        for a in range(KP):
+            load_words(1, a)
+        load_dealt(nc.sync, wg1_sb[3], wg1, 3, 4)
+        load_page(3)
+        load_dealt(nc.sync, wg2_first, wg2, 0, 1)
+        load_list("offs4", offs4)
+        load_dealt(nc.sync, wg2_rest, wg2, 1, PACK)
+        load_list("offs5", offs5)
+        load_page(4)
+        load_page(5)
+
+        for a in range(KP):
+            quantize_w1(0, a)
+        for a in range(KP):
+            load_w1(1, a)
+        load_rowvec(nc.sync, lvl_sb, lvl)
+        load_page(6)
+        load_page(7)
+        nc.sync.dma_start(w4c[:].bitcast(I32), w4_words.rearrange("b p n -> p b n").bitcast(I32))
+        with nc.allow_non_contiguous_dma(reason="one gain value for each partition"):
+            nc.sync.dma_start(gain_sb[:], gain.rearrange("(c p) -> p c", p=P))
+
+        gather_table(0)
+        put(0, 0)
+        put(0, 1)
+        put(0, 2)
+        gather_table(1)
+        put(0, 3)
+        put(1, 0)
+        put(1, 1)
+        put(1, 2)
+        put(1, 3)
+        for a in range(KP):
+            quantize_w1(1, a)
+            fetch(a)
+
+        nc.scalar.mul(neg_lvl[:], lvl_sb[:], -1.0)
+        put(0, 4)
+        put(0, 5)
+        level(0)
+        fetch(3)
+        put(1, 4)
+        put(1, 5)
+        level(1)
+        fetch(4)
+        put(0, 6)
+        level(2)
+        fetch(5)
+        put(1, 6)
+        put(0, 7)
+        level(3)
+        fetch(6)
+        quantize_x(0)
+        put(1, 7)
+        for u in (4, 5, 6):
+            level(u)
+
+        units = [(m0, QUARTER, (n, n + 1)) for m0 in (0, QUARTER) for n in range(0, NT, 2)]
+        units = units + [(HALF, HALF, (n,)) for n in range(NT)]
+        for i in range(BANKS):
+            score(banks[i], 0, units[i])
+        fetch(7, 0, QUARTER, at=0)
+        level(7, 0, QUARTER, at=0)
+        fetch(7, QUARTER, HALF, at=HALF)
+        level(7, QUARTER, HALF, at=HALF)
+        quantize_x(1, 0, QUARTER)
+        fetch(7, HALF, PICK, at=0)
+        quantize_x(1, QUARTER, HALF)
+        level(7, HALF, PICK, at=0)
+        quantize_x(1, HALF, PICK)
+
+        staged = [tile([P, PICK], F32, "staged%d" % n, tag="page%d" % n) for n in range(NT)]
+        for i, unit in enumerate(units):
+            m0, width, ns = unit
+            bank = banks[i % BANKS]
+            if i >= BANKS:
+                score(bank, 0, unit)
+            score(bank, 1, unit)
+            stage = staged[i % NT][:, (i // NT) * HALF:(i // NT + 1) * HALF]
+            for k, n in enumerate(ns):
+                cols = slice(k * width, (k + 1) * width)
+                if i in ON_VECTOR:
+                    nc.vector.tensor_scalar(stage[:, cols], bank[:, cols], gain_sb[:, n:n + 1], None, ALU.mult)
+                else:
+                    nc.scalar.activation(stage[:, cols], bank[:, cols], ACT.Copy, scale=gain_sb[:, n:n + 1])
+            rows = out[ns[0] * P:(ns[-1] + 1) * P, m0:m0 + width]
+            nc.sync.dma_start(rows.rearrange("(k p) m -> p k m", p=P), stage.rearrange("p (k m) -> p k m", m=width))

@@ -26,7 +26,8 @@ HALF = 512
 RING = 6
 QUARTER = 256
 BANKS = 8
-ON_VECTOR = (0, 1, 2, 4, 6, 8, 10)
+LATE = 3
+ON_VECTOR = (0, 1, 2, 6, 8, 10)
 
 
 def tile_list_banknote_fitness_archive_kernel(
@@ -85,10 +86,10 @@ def tile_list_banknote_fitness_archive_kernel(
             src = (tab_words, tab2_words)[s]
             nc.sync.dma_start(words[s][a][:].bitcast(I32), src[a].rearrange("p t i -> p (t i)").bitcast(I32))
 
-        def load_scales(eng, s):
+        def load_scales(s, quadrants):
             src = (tab_scales, tab2_scales)[s]
-            for q in range(4):
-                eng.dma_start(scale_win[s][32 * q:32 * q + 4 * KP, :].bitcast(I32),
+            for q in quadrants:
+                nc.sync.dma_start(scale_win[s][32 * q:32 * q + 4 * KP, :].bitcast(I32),
                                     src[:, 4 * q:4 * q + 4, :].bitcast(I32))
 
         def load_page(u):
@@ -171,37 +172,36 @@ def tile_list_banknote_fitness_archive_kernel(
             nc.vector.memset(scale_win[s][:].bitcast(I32), 0)
         nc.vector.memset(w4s[:].rearrange("p b n -> p (b n)").bitcast(I32), 0)
 
-        load_scales(nc.gpsimd, 0)
-        load_rowvec(nc.gpsimd, rowgain[0], gf)
-        load_scales(nc.gpsimd, 1)
-        load_rowvec(nc.gpsimd, rowgain[1], gb)
-        for q in range(4):
-            nc.gpsimd.dma_start(w4s[32 * q:32 * q + 4, :, :].bitcast(I32),
-                                w4_scales[:, 4 * q:4 * q + 4, :].rearrange("b r n -> r b n").bitcast(I32))
-
         load_w1(0, 0)
         load_list("offs", offs)
+        load_rowvec(nc.sync, rowgain[0], gf)
         load_w1(0, 1)
-        load_list("offs3", offs3)
-        load_w1(0, 2)
         load_list("offs2", offs2)
+        load_list("offs3", offs3)
+        load_rowvec(nc.sync, rowgain[1], gb)
+        load_w1(0, 2)
+        load_scales(0, (0, 1, 2,))
         load_words(0, 0)
-        load_words(0, 1)
-        load_words(0, 2)
+        load_scales(0, (3,))
         load_dealt(nc.sync, wg1_sb[0], wg1, 0, 1)
+        load_words(0, 1)
+        load_scales(1, (0, 1, 2, 3,))
+        load_words(0, 2)
         load_page(0)
-        for t in (1, 2):
-            load_dealt(nc.sync, wg1_sb[t], wg1, t, t + 1)
-            load_page(t)
-        for a in range(KP):
-            load_words(1, a)
+        load_dealt(nc.sync, wg1_sb[1], wg1, 1, 2)
+        load_page(1)
+        load_dealt(nc.sync, wg1_sb[2], wg1, 2, 3)
+        load_page(2)
+        load_list("offs4", offs4)
+        load_words(1, 0)
         load_dealt(nc.sync, wg1_sb[3], wg1, 3, 4)
+        load_words(1, 1)
+        load_words(1, 2)
         load_page(3)
         load_dealt(nc.sync, wg2_first, wg2, 0, 1)
-        load_list("offs4", offs4)
         load_dealt(nc.sync, wg2_rest, wg2, 1, PACK)
-        load_list("offs5", offs5)
         load_page(4)
+        load_list("offs5", offs5)
         load_page(5)
 
         for a in range(KP):
@@ -212,6 +212,9 @@ def tile_list_banknote_fitness_archive_kernel(
         load_page(6)
         load_page(7)
         nc.sync.dma_start(w4c[:].bitcast(I32), w4_words.rearrange("b p n -> p b n").bitcast(I32))
+        for q in range(4):
+            nc.sync.dma_start(w4s[32 * q:32 * q + 4, :, :].bitcast(I32),
+                              w4_scales[:, 4 * q:4 * q + 4, :].rearrange("b r n -> r b n").bitcast(I32))
         with nc.allow_non_contiguous_dma(reason="one gain value for each partition"):
             nc.sync.dma_start(gain_sb[:], gain.rearrange("(c p) -> p c", p=P))
 
@@ -262,10 +265,11 @@ def tile_list_banknote_fitness_archive_kernel(
         fetch(7, HALF, PICK, at=0)
         quantize_x(1, QUARTER, HALF)
         level(7, HALF, PICK, at=0)
-        quantize_x(1, HALF, PICK)
 
         staged = [tile([P, PICK], F32, "staged%d" % n, tag="page%d" % n) for n in range(NT)]
         for i, unit in enumerate(units):
+            if i == LATE:
+                quantize_x(1, HALF, PICK)
             m0, width, ns = unit
             bank = banks[i % BANKS]
             if i >= BANKS:

@@ -26,6 +26,7 @@ HALF = 512
 RING = 6
 QUARTER = 256
 BANKS = 8
+DIRECT = 6
 LATE = 3
 ON_VECTOR = (0, 1, 2, 6, 8, 10)
 
@@ -86,10 +87,10 @@ def tile_list_banknote_fitness_archive_kernel(
             src = (tab_words, tab2_words)[s]
             nc.sync.dma_start(words[s][a][:].bitcast(I32), src[a].rearrange("p t i -> p (t i)").bitcast(I32))
 
-        def load_scales(s, quadrants):
+        def load_scales(s, quadrants, eng=nc.sync):
             src = (tab_scales, tab2_scales)[s]
             for q in quadrants:
-                nc.sync.dma_start(scale_win[s][32 * q:32 * q + 4 * KP, :].bitcast(I32),
+                eng.dma_start(scale_win[s][32 * q:32 * q + 4 * KP, :].bitcast(I32),
                                     src[:, 4 * q:4 * q + 4, :].bitcast(I32))
 
         def load_page(u):
@@ -104,11 +105,12 @@ def tile_list_banknote_fitness_archive_kernel(
         def load_rowvec(eng, dst, src):
             eng.dma_start(dst[:], src.rearrange("(b p t) -> p b t", b=HB, t=PACK))
 
-        def quantize_w1(b, a):
-            g = grouped[a]
-            nc.scalar.copy(g[:].rearrange("p (t m j) -> p m j t", t=PACK, j=PACK),
-                           raw[a][:].rearrange("p (j m t) -> p m j t", j=PACK, t=PACK))
-            nc.vector.quantize_mx(out=w1_codes[b][a][:].bitcast(FP8X4), scales=w1_scales[b][a][:], in_=g[:])
+        def quantize_w1(b, a, t0=0, t1=PACK, cast=nc.scalar.copy):
+            cast(grouped[a][:].rearrange("p (t m j) -> p t m j", t=PACK, j=PACK)[:, t0:t1],
+                 raw[a][:].rearrange("p (j m t) -> p t m j", j=PACK, t=PACK)[:, t0:t1])
+            cols = slice(t0 * P, t1 * P)
+            nc.vector.quantize_mx(out=w1_codes[b][a][:, cols].bitcast(FP8X4), scales=w1_scales[b][a][:, cols],
+                                  in_=grouped[a][:, t0 * PASS:t1 * PASS])
 
         def gather_table(s):
             lst = lists[("offs", "offs2")[s]]
@@ -140,14 +142,22 @@ def tile_list_banknote_fitness_archive_kernel(
             at = m0 if at is None else at
             nc.vector.tensor_copy(raw[u % KP][:, at:at + m1 - m0], pages[u][:].indirect(lists["offs5"][:, m0 // 16:m1 // 16]))
 
+        planes = tile([P, PACK * PICK], BF16, "planes", tag="words02")
+        for b in range(HB):
+            woven[b] = tile([P, PICK * PACK], BF16, "woven%d" % b, tag="words0%d" % b)
+
         def level(u, m0=0, m1=PICK, at=None):
             at = m0 if at is None else at
             b, t = divmod(u, PACK)
-            if b not in woven:
-                woven[b] = tile([P, PICK * PACK], BF16, "woven%d" % b, tag="words0%d" % b)
-            nc.scalar.activation(
-                woven[b][:].rearrange("p (m t) -> p m t", t=PACK)[:, m0:m1, t],
-                raw[u % KP][:, at:at + m1 - m0], ACT.Identity, bias=neg_lvl[:, b, t:t + 1])
+            if u < DIRECT:
+                dst = planes[:, t * PICK:(t + 1) * PICK]
+            else:
+                dst = woven[b][:].rearrange("p (m t) -> p m t", t=PACK)[:, m0:m1, t]
+            nc.scalar.activation(dst, raw[u % KP][:, at:at + m1 - m0], ACT.Identity, bias=neg_lvl[:, b, t:t + 1])
+
+        def weave(b, count):
+            nc.scalar.copy(woven[b][:].rearrange("p (m t) -> p m t", t=PACK)[:, :, 0:count],
+                           planes[:].rearrange("p (t m) -> p m t", t=PACK)[:, :, 0:count])
 
         def quantize_x(b, m0=0, m1=PICK):
             nc.vector.quantize_mx(out=x_codes[b][:, m0:m1].bitcast(FP8X4), scales=x_scales[b][:, m0:m1],
@@ -169,29 +179,29 @@ def tile_list_banknote_fitness_archive_kernel(
         nc.vector.memset(zero_in[:], 0.0)
         nc.scalar.activation(zero[:], zero_in[:], ACT.Tanh)
         for s in range(2):
-            nc.vector.memset(scale_win[s][:].bitcast(I32), 0)
+            (nc.gpsimd, nc.vector)[s].memset(scale_win[s][:].bitcast(I32), 0)
+        load_scales(0, range(4), nc.gpsimd)
         nc.vector.memset(w4s[:].rearrange("p b n -> p (b n)").bitcast(I32), 0)
 
         load_w1(0, 0)
-        load_list("offs", offs)
-        load_rowvec(nc.sync, rowgain[0], gf)
-        load_w1(0, 1)
-        load_list("offs2", offs2)
         load_list("offs3", offs3)
-        load_rowvec(nc.sync, rowgain[1], gb)
+        load_w1(0, 1)
+        load_rowvec(nc.sync, rowgain[0], gf)
         load_w1(0, 2)
-        load_scales(0, (0, 1, 2,))
+        load_list("offs2", offs2)
         load_words(0, 0)
-        load_scales(0, (3,))
+        load_list("offs", offs)
         load_dealt(nc.sync, wg1_sb[0], wg1, 0, 1)
         load_words(0, 1)
-        load_scales(1, (0, 1, 2, 3,))
+        load_rowvec(nc.sync, rowgain[1], gb)
         load_words(0, 2)
         load_page(0)
         load_dealt(nc.sync, wg1_sb[1], wg1, 1, 2)
         load_page(1)
+        load_scales(1, (0, 1,))
         load_dealt(nc.sync, wg1_sb[2], wg1, 2, 3)
         load_page(2)
+        load_scales(1, (2, 3,))
         load_list("offs4", offs4)
         load_words(1, 0)
         load_dealt(nc.sync, wg1_sb[3], wg1, 3, 4)
@@ -202,13 +212,14 @@ def tile_list_banknote_fitness_archive_kernel(
         load_dealt(nc.sync, wg2_rest, wg2, 1, PACK)
         load_page(4)
         load_list("offs5", offs5)
-        load_page(5)
-
         for a in range(KP):
-            quantize_w1(0, a)
+            quantize_w1(0, a, 0, 2, nc.vector.tensor_copy)
+        for a in range(KP):
+            quantize_w1(0, a, 2, PACK)
         for a in range(KP):
             load_w1(1, a)
         load_rowvec(nc.sync, lvl_sb, lvl)
+        load_page(5)
         load_page(6)
         load_page(7)
         nc.sync.dma_start(w4c[:].bitcast(I32), w4_words.rearrange("b p n -> p b n").bitcast(I32))
@@ -245,13 +256,16 @@ def tile_list_banknote_fitness_archive_kernel(
         level(2)
         fetch(5)
         put(1, 6)
-        put(0, 7)
         level(3)
+        weave(0, PACK)
         fetch(6)
+        put(0, 7)
         quantize_x(0)
         put(1, 7)
-        for u in (4, 5, 6):
-            level(u)
+        level(4)
+        level(5)
+        weave(1, 2)
+        level(6)
 
         units = [(m0, QUARTER, (n, n + 1)) for m0 in (0, QUARTER) for n in range(0, NT, 2)]
         units = units + [(HALF, HALF, (n,)) for n in range(NT)]

@@ -1,6 +1,7 @@
 from contextlib import ExitStack
 
 import concourse.mybir as mybir
+from concourse.masks import make_identity
 
 K, T, S, H, T2, PICK, N = 1536, 2048, 512, 1024, 2048, 1024, 768
 FLOPS = 2 * (2 * K * H * S + H * N * PICK)
@@ -58,14 +59,11 @@ def tile_list_banknote_fitness_archive_kernel(
         scale_win = [tile([P, T], U8, "scalewin%d" % s) for s in range(2)]
         v_codes = [[tile([P, S], U32, "vc%d%d" % (s, a)) for a in range(KP)] for s in range(2)]
         v_scales = [tile([P, S], U8, "vs%d" % s) for s in range(2)]
+        spread = [tile([P, PACK * S], F32, "spread%d" % s, tag="page%d" % (7 - s)) for s in range(2)]
         pages = [tile([P, T2], F32, "page%d" % u) for u in range(HB * PACK)]
-        wg1_sb = [tile([P, S], F32, "wg1_%d" % t) for t in range(PACK)]
-        wg2_first = tile([P, S], F32, "wg2_first")
-        wg2_rest = tile([P, (PACK - 1) * S], F32, "wg2_rest")
-        dealt = [[wg1_sb[t][:] for t in range(PACK)],
-                 [wg2_first[:]] + [wg2_rest[:, t * S:(t + 1) * S] for t in range(PACK - 1)]]
-        first = [[tile([P, S], F32, "factor%d%d" % (s, t)) for t in range(PACK)] for s in range(2)]
-        factor = [[first[s][t][:] for t in range(PACK)] + dealt[s] for s in range(2)]
+        wg_rows = [tile([P, S], F32, "wg_rows%d" % s) for s in range(2)]
+        factor = [[tile([P, S], F32, "factor%d%d" % (s, u)) for u in range(HB * PACK)] for s in range(2)]
+        identity = tile([P, P], F32, "identity")
         feat = [tile([P, S], F32, "feat%d" % i) for i in range(RING)]
         w4c = tile([P, HB, 2 * N], U8, "w4c")
         w4s = tile([P, HB, N], U8, "w4s")
@@ -97,10 +95,22 @@ def tile_list_banknote_fitness_archive_kernel(
             b, t = divmod(u, PACK)
             nc.sync.dma_start(pages[u][:], page0.rearrange("(b p t) c -> b t p c", b=HB, t=PACK)[b, t])
 
-        def load_dealt(eng, dst, src, t0, t1):
-            rows = src.rearrange("(q t) j -> q (t j)", t=PACK)[:, t0 * S:t1 * S]
-            for q in range(4):
-                eng.dma_start(dst[32 * q:32 * q + 32, :], rows)
+        def make_factors(s):
+            turned = banks[7]
+            for c in range(S // P):
+                cols = slice(c * P, (c + 1) * P)
+                nc.tensor.transpose(turned[:, cols], wg_rows[s][:, cols], identity[:])
+            for t in range(PACK):
+                picked = turned[:].rearrange("j (c q t) -> j t c q", c=S // P, t=PACK)[:, t]
+                nc.scalar.copy(spread[s][:, t * S:(t + 1) * S].rearrange("j (c r q) -> j c r q", c=S // P, r=4),
+                               picked.unsqueeze(2).to_broadcast([P, S // P, 4, 32]))
+                for c in range(S // P):
+                    nc.tensor.transpose(banks[6 - t][:, c * P:(c + 1) * P],
+                                        spread[s][:, t * S + c * P:t * S + (c + 1) * P], identity[:])
+            for b in range(HB):
+                for t in range(PACK):
+                    nc.scalar.activation(factor[s][PACK * b + t][:], banks[6 - t][:], ACT.Copy,
+                                         scale=rowgain[s][:, b, t:t + 1])
 
         def load_rowvec(eng, dst, src):
             eng.dma_start(dst[:], src.rearrange("(b p t) -> p b t", b=HB, t=PACK))
@@ -131,10 +141,9 @@ def tile_list_banknote_fitness_archive_kernel(
                     out=bank[:], lhsT=w1_codes[b][a][:, cols].bitcast(FP8X4), lhsT_scale=w1_scales[b][a][:, cols],
                     rhs=v_codes[s][a][:].bitcast(FP8X4), rhs_scale=v_scales[s][4 * a:P, :],
                     start=(a == 0), stop=(a == KP - 1))
-            nc.scalar.activation(factor[s][u], dealt[s][t], ACT.Copy, scale=rowgain[s][:, b, t:t + 1])
             nc.scalar.activation(feat[n % RING][:], bank[:], (ACT.Tanh, ACT.Square)[s], bias=zero[:])
             lst = lists[("offs3", "offs4")[s]]
-            nc.vector.tensor_tensor(pages[u][:].indirect(lst[:]), feat[n % RING][:], factor[s][u], ALU.mult)
+            nc.vector.tensor_tensor(pages[u][:].indirect(lst[:]), feat[n % RING][:], factor[s][u][:], ALU.mult)
 
         woven = {}
 
@@ -180,36 +189,32 @@ def tile_list_banknote_fitness_archive_kernel(
         nc.scalar.activation(zero[:], zero_in[:], ACT.Tanh)
         for s in range(2):
             (nc.gpsimd, nc.vector)[s].memset(scale_win[s][:].bitcast(I32), 0)
+        make_identity(nc, identity[:])
         load_scales(0, range(4), nc.gpsimd)
+        load_scales(1, range(4), nc.gpsimd)
         nc.vector.memset(w4s[:].rearrange("p b n -> p (b n)").bitcast(I32), 0)
 
         load_w1(0, 0)
-        load_list("offs3", offs3)
-        load_w1(0, 1)
         load_rowvec(nc.sync, rowgain[0], gf)
+        load_w1(0, 1)
+        load_list("offs3", offs3)
         load_w1(0, 2)
-        load_list("offs2", offs2)
+        nc.sync.dma_start(wg_rows[0][:], wg1)
         load_words(0, 0)
         load_list("offs", offs)
-        load_dealt(nc.sync, wg1_sb[0], wg1, 0, 1)
         load_words(0, 1)
         load_rowvec(nc.sync, rowgain[1], gb)
         load_words(0, 2)
+        load_list("offs2", offs2)
         load_page(0)
-        load_dealt(nc.sync, wg1_sb[1], wg1, 1, 2)
+        nc.sync.dma_start(wg_rows[1][:], wg2)
         load_page(1)
-        load_scales(1, (0, 1,))
-        load_dealt(nc.sync, wg1_sb[2], wg1, 2, 3)
         load_page(2)
-        load_scales(1, (2, 3,))
-        load_list("offs4", offs4)
         load_words(1, 0)
-        load_dealt(nc.sync, wg1_sb[3], wg1, 3, 4)
         load_words(1, 1)
         load_words(1, 2)
         load_page(3)
-        load_dealt(nc.sync, wg2_first, wg2, 0, 1)
-        load_dealt(nc.sync, wg2_rest, wg2, 1, PACK)
+        load_list("offs4", offs4)
         load_page(4)
         load_list("offs5", offs5)
         for a in range(KP):
@@ -220,6 +225,13 @@ def tile_list_banknote_fitness_archive_kernel(
             load_w1(1, a)
         load_rowvec(nc.sync, lvl_sb, lvl)
         load_page(5)
+
+        make_factors(0)
+        gather_table(0)
+        put(0, 0)
+        put(0, 1)
+        put(0, 2)
+        make_factors(1)
         load_page(6)
         load_page(7)
         nc.sync.dma_start(w4c[:].bitcast(I32), w4_words.rearrange("b p n -> p b n").bitcast(I32))
@@ -229,10 +241,6 @@ def tile_list_banknote_fitness_archive_kernel(
         with nc.allow_non_contiguous_dma(reason="one gain value for each partition"):
             nc.sync.dma_start(gain_sb[:], gain.rearrange("(c p) -> p c", p=P))
 
-        gather_table(0)
-        put(0, 0)
-        put(0, 1)
-        put(0, 2)
         gather_table(1)
         put(0, 3)
         put(1, 0)

@@ -22,14 +22,17 @@ PACK = 4
 PASS = P * PACK
 KP = K // PASS
 HB = H // PASS
+TILES = HB * PACK
+LAST = TILES - 1
 NT = N // P
-HALF = 512
-RING = 6
-QUARTER = 256
 BANKS = 8
-DIRECT = 6
-LATE = 3
-ON_VECTOR = (0, 1, 2, 6, 8, 10)
+HALF = 512
+QUARTER = 256
+QUADRANTS = 4
+FEATS = 6
+PLANAR = 6
+VECTOR_CASTS = 2
+FRONT, BACK = 0, 1
 
 
 def tile_list_banknote_fitness_archive_kernel(
@@ -44,265 +47,287 @@ def tile_list_banknote_fitness_archive_kernel(
         def tile(shape, dtype, name, tag=None):
             return sb.tile(shape, dtype, name=name, tag=tag or name, align_bytes=64)
 
-        lists = {}
-
-        def load_list(name, ap):
-            lists[name] = tile([P, ap.shape[1]], U16, "list_" + name)
-            nc.sync.dma_start(lists[name][:], ap)
-
         banks = [ps.tile([P, HALF], F32, name="bank%d" % i, tag="bank%d" % i) for i in range(BANKS)]
-        raw = [tile([P, PACK * PASS], F32, "raw%d" % a) for a in range(KP)]
-        grouped = [tile([P, PACK * PASS], BF16, "grouped%d" % i) for i in range(KP)]
+        staging = [tile([P, PACK * PASS], F32, "staging%d" % a) for a in range(KP)]
+        grouped = [tile([P, PACK * PASS], BF16, "grouped%d" % a) for a in range(KP)]
         w1_codes = [[tile([P, PASS], U32, "w1c%d%d" % (b, a)) for a in range(KP)] for b in range(HB)]
         w1_scales = [[tile([P, PASS], U8, "w1s%d%d" % (b, a)) for a in range(KP)] for b in range(HB)]
-        words = [[tile([P, T], U32, "words%d%d" % (s, a)) for a in range(KP)] for s in range(2)]
-        scale_win = [tile([P, T], U8, "scalewin%d" % s) for s in range(2)]
-        v_codes = [[tile([P, S], U32, "vc%d%d" % (s, a)) for a in range(KP)] for s in range(2)]
-        v_scales = [tile([P, S], U8, "vs%d" % s) for s in range(2)]
-        spread = [tile([P, PACK * S], F32, "spread%d" % s, tag="page%d" % (7 - s)) for s in range(2)]
-        pages = [tile([P, T2], F32, "page%d" % u) for u in range(HB * PACK)]
-        wg_rows = [tile([P, S], F32, "wg_rows%d" % s) for s in range(2)]
-        factor = [[tile([P, S], F32, "factor%d%d" % (s, u)) for u in range(HB * PACK)] for s in range(2)]
+        words = [[tile([P, T], U32, "words%d%d" % (s, a)) for a in range(KP)] for s in (FRONT, BACK)]
+        table_scales = [tile([P, T], U8, "table_scales%d" % s) for s in (FRONT, BACK)]
+        v_codes = [[tile([P, S], U32, "vc%d%d" % (s, a)) for a in range(KP)] for s in (FRONT, BACK)]
+        spread = [tile([P, PACK * S], F32, "spread%d" % s, tag="page%d" % (LAST - s)) for s in (FRONT, BACK)]
+        pages = [tile([P, T2], F32, "page%d" % u) for u in range(TILES)]
+        wg_rows = [tile([P, S], F32, "wg_rows%d" % s) for s in (FRONT, BACK)]
+        factor = [[tile([P, S], F32, "factor%d%d" % (s, u)) for u in range(TILES)] for s in (FRONT, BACK)]
+        v_scales = [tile([P, S], U8, "vs%d" % s) for s in (FRONT, BACK)]
         identity = tile([P, P], F32, "identity")
-        feat = [tile([P, S], F32, "feat%d" % i) for i in range(RING)]
+        feat = [tile([P, S], F32, "feat%d" % i) for i in range(FEATS)]
         w4c = tile([P, HB, 2 * N], U8, "w4c")
         w4s = tile([P, HB, N], U8, "w4s")
-        rowgain = [tile([P, HB, PACK], F32, "rowgain%d" % s) for s in range(2)]
+        gf_sb = [tile([P, PACK], F32, "gf_sb%d" % b) for b in range(HB)]
+        gb_sb = tile([P, HB, PACK], F32, "gb_sb")
+        row_gain = [[gf_sb[b][:] for b in range(HB)], [gb_sb[:, b] for b in range(HB)]]
         lvl_sb = tile([P, HB, PACK], F32, "lvl_sb")
         neg_lvl = tile([P, HB, PACK], F32, "neg_lvl")
         gain_sb = tile([P, NT], F32, "gain_sb")
         zero_in = tile([P, 1], F32, "zero_in")
         zero = tile([P, 1], F32, "zero")
-        x_codes = [tile([P, PICK], U32, "xc%d" % b, tag="words1%d" % b) for b in range(HB)]
+        x_codes = {(0, 0): tile([P, HALF], U32, "xc00", tag="words10")[:]}
+        last_codes = tile([P, PICK], U32, "xc1", tag="words11")
+        x_codes[1, 0], x_codes[1, 1] = last_codes[:, 0:HALF], last_codes[:, HALF:PICK]
         x_scales = [tile([P, PICK], U8, "xs%d" % b) for b in range(HB)]
+        planes = tile([P, PACK * PICK], BF16, "planes", tag="words02")
+        woven = [tile([P, PICK * PACK], BF16, "woven%d" % b, tag="words0%d" % b) for b in range(HB)]
+        lists = {}
+        done_puts = []
+
+        def load_list(name, src):
+            lists[name] = tile([P, src.shape[1]], U16, "list_" + name)
+            nc.sync.dma_start(lists[name][:], src)
 
         def load_w1(b, a):
             nc.sync.dma_start(
-                raw[a][:].rearrange("p (j c) -> p j c", j=PACK),
+                staging[a][:].rearrange("p (j c) -> p j c", j=PACK),
                 w1[a * PASS:(a + 1) * PASS, b * PASS:(b + 1) * PASS].rearrange("(p j) c -> p j c", j=PACK))
 
         def load_words(s, a):
             src = (tab_words, tab2_words)[s]
             nc.sync.dma_start(words[s][a][:].bitcast(I32), src[a].rearrange("p t i -> p (t i)").bitcast(I32))
 
-        def load_scales(s, quadrants, eng=nc.sync):
+        def load_table_scales(s):
             src = (tab_scales, tab2_scales)[s]
-            for q in quadrants:
-                eng.dma_start(scale_win[s][32 * q:32 * q + 4 * KP, :].bitcast(I32),
+            for q in range(QUADRANTS):
+                nc.gpsimd.dma_start(table_scales[s][32 * q:32 * q + 4 * KP, :].bitcast(I32),
                                     src[:, 4 * q:4 * q + 4, :].bitcast(I32))
 
         def load_page(u):
             b, t = divmod(u, PACK)
             nc.sync.dma_start(pages[u][:], page0.rearrange("(b p t) c -> b t p c", b=HB, t=PACK)[b, t])
 
-        def make_factors(s):
-            turned = banks[7]
+        def load_gf(b):
+            nc.sync.dma_start(gf_sb[b][:], gf[b * PASS:(b + 1) * PASS].rearrange("(p t) -> p t", t=PACK))
+
+        def load_by_row(dst, src):
+            nc.sync.dma_start(dst[:], src.rearrange("(b p t) -> p b t", b=HB, t=PACK))
+
+        turned = banks[7]
+        dealt = [banks[6], banks[5], banks[4], turned]
+
+        def deal_wg(s):
             for c in range(S // P):
                 cols = slice(c * P, (c + 1) * P)
                 nc.tensor.transpose(turned[:, cols], wg_rows[s][:, cols], identity[:])
             for t in range(PACK):
                 picked = turned[:].rearrange("j (c q t) -> j t c q", c=S // P, t=PACK)[:, t]
-                nc.scalar.copy(spread[s][:, t * S:(t + 1) * S].rearrange("j (c r q) -> j c r q", c=S // P, r=4),
-                               picked.unsqueeze(2).to_broadcast([P, S // P, 4, 32]))
+                nc.scalar.copy(
+                    spread[s][:, t * S:(t + 1) * S].rearrange("j (c r q) -> j c r q", c=S // P, r=PACK),
+                    picked.unsqueeze(2).to_broadcast([P, S // P, PACK, P // PACK]))
                 for c in range(S // P):
-                    nc.tensor.transpose(banks[6 - t][:, c * P:(c + 1) * P],
+                    nc.tensor.transpose(dealt[t][:, c * P:(c + 1) * P],
                                         spread[s][:, t * S + c * P:t * S + (c + 1) * P], identity[:])
-            for b in range(HB):
-                for t in range(PACK):
-                    nc.scalar.activation(factor[s][PACK * b + t][:], banks[6 - t][:], ACT.Copy,
-                                         scale=rowgain[s][:, b, t:t + 1])
 
-        def load_rowvec(eng, dst, src):
-            eng.dma_start(dst[:], src.rearrange("(b p t) -> p b t", b=HB, t=PACK))
+        def make_factors(s, b):
+            for t in range(PACK):
+                nc.scalar.activation(factor[s][PACK * b + t][:], dealt[t][:], ACT.Copy,
+                                     scale=row_gain[s][b][:, t:t + 1])
 
         def quantize_w1(b, a, t0=0, t1=PACK, cast=nc.scalar.copy):
             cast(grouped[a][:].rearrange("p (t m j) -> p t m j", t=PACK, j=PACK)[:, t0:t1],
-                 raw[a][:].rearrange("p (j m t) -> p t m j", j=PACK, t=PACK)[:, t0:t1])
+                 staging[a][:].rearrange("p (j m t) -> p t m j", j=PACK, t=PACK)[:, t0:t1])
             cols = slice(t0 * P, t1 * P)
             nc.vector.quantize_mx(out=w1_codes[b][a][:, cols].bitcast(FP8X4), scales=w1_scales[b][a][:, cols],
                                   in_=grouped[a][:, t0 * PASS:t1 * PASS])
 
         def gather_table(s):
-            lst = lists[("offs", "offs2")[s]]
-            nc.vector.tensor_copy(v_scales[s][:], scale_win[s][:].indirect(lst[:]))
+            offsets = lists[("offs", "offs2")[s]]
+            nc.vector.tensor_copy(v_scales[s][:], table_scales[s][:].indirect(offsets[:]))
             for a in range(KP):
-                nc.vector.tensor_copy(v_codes[s][a][:], words[s][a][:].indirect(lst[:]))
-
-        puts = []
+                nc.vector.tensor_copy(v_codes[s][a][:], words[s][a][:].indirect(offsets[:]))
 
         def put(s, u):
-            n = len(puts)
-            puts.append((s, u))
+            count = len(done_puts)
+            done_puts.append((s, u))
             b, t = divmod(u, PACK)
-            bank = banks[n % BANKS]
+            bank = banks[t if b == 0 else count % BANKS]
             cols = slice(t * P, (t + 1) * P)
             for a in range(KP):
                 nc.tensor.matmul_mx(
                     out=bank[:], lhsT=w1_codes[b][a][:, cols].bitcast(FP8X4), lhsT_scale=w1_scales[b][a][:, cols],
                     rhs=v_codes[s][a][:].bitcast(FP8X4), rhs_scale=v_scales[s][4 * a:P, :],
                     start=(a == 0), stop=(a == KP - 1))
-            nc.scalar.activation(feat[n % RING][:], bank[:], (ACT.Tanh, ACT.Square)[s], bias=zero[:])
-            lst = lists[("offs3", "offs4")[s]]
-            nc.vector.tensor_tensor(pages[u][:].indirect(lst[:]), feat[n % RING][:], factor[s][u][:], ALU.mult)
+            features = feat[count % FEATS]
+            nc.scalar.activation(features[:], bank[:], (ACT.Tanh, ACT.Square)[s], bias=zero[:])
+            offsets = lists[("offs3", "offs4")[s]]
+            nc.vector.tensor_tensor(pages[u][:].indirect(offsets[:]), features[:], factor[s][u][:], ALU.mult)
 
-        woven = {}
+        def fetch(u, dst, m0=0, m1=PICK):
+            nc.vector.tensor_copy(dst, pages[u][:].indirect(lists["offs5"][:, m0 // 16:m1 // 16]))
 
-        def fetch(u, m0=0, m1=PICK, at=None):
-            at = m0 if at is None else at
-            nc.vector.tensor_copy(raw[u % KP][:, at:at + m1 - m0], pages[u][:].indirect(lists["offs5"][:, m0 // 16:m1 // 16]))
-
-        planes = tile([P, PACK * PICK], BF16, "planes", tag="words02")
-        for b in range(HB):
-            woven[b] = tile([P, PICK * PACK], BF16, "woven%d" % b, tag="words0%d" % b)
-
-        def level(u, m0=0, m1=PICK, at=None):
-            at = m0 if at is None else at
+        def level(u, src, m0=0, m1=PICK):
             b, t = divmod(u, PACK)
-            if u < DIRECT:
+            if u < PLANAR:
                 dst = planes[:, t * PICK:(t + 1) * PICK]
             else:
                 dst = woven[b][:].rearrange("p (m t) -> p m t", t=PACK)[:, m0:m1, t]
-            nc.scalar.activation(dst, raw[u % KP][:, at:at + m1 - m0], ACT.Identity, bias=neg_lvl[:, b, t:t + 1])
+            nc.scalar.activation(dst, src, ACT.Identity, bias=neg_lvl[:, b, t:t + 1])
+
+        def fetched(u):
+            return staging[u % KP][:, 0:PICK]
 
         def weave(b, count):
             nc.scalar.copy(woven[b][:].rearrange("p (m t) -> p m t", t=PACK)[:, :, 0:count],
                            planes[:].rearrange("p (t m) -> p m t", t=PACK)[:, :, 0:count])
 
-        def quantize_x(b, m0=0, m1=PICK):
-            nc.vector.quantize_mx(out=x_codes[b][:, m0:m1].bitcast(FP8X4), scales=x_scales[b][:, m0:m1],
+        def codes_of(b, m0, m1):
+            half, start = divmod(m0, HALF)
+            return x_codes[b, half][:, start:start + m1 - m0].bitcast(FP8X4)
+
+        def quantize_x(b, m0, m1):
+            nc.vector.quantize_mx(out=codes_of(b, m0, m1), scales=x_scales[b][:, m0:m1],
                                   in_=woven[b][:, PACK * m0:PACK * m1])
 
-        def score(bank, b, unit):
-            m0, width, ns = unit
+        early = [(m0, QUARTER, (n, n + 1)) for m0 in (0, QUARTER) for n in range(0, NT, 2)]
+        units = early + [(HALF, HALF, (n,)) for n in range(NT)]
+
+        def score(i, b):
+            m0, width, row_tiles = units[i]
             step = HALF if width == HALF else P
-            passes = [(i, n, c) for i, n in enumerate(ns) for c in range(0, width, step)]
-            for k, (i, n, c) in enumerate(passes):
+            pieces = [(k, n, c) for k, n in enumerate(row_tiles) for c in range(0, width, step)]
+            for j, (k, n, c) in enumerate(pieces):
                 nc.tensor.matmul_mx(
-                    out=bank[:, i * width + c:i * width + c + step],
+                    out=banks[i % BANKS][:, k * width + c:k * width + c + step],
                     lhsT=w4c[:, b, 2 * P * n:2 * P * (n + 1)].bitcast(FP4X4),
                     lhsT_scale=w4s[:, b, P * n:P * (n + 1)],
-                    rhs=x_codes[b][:, m0 + c:m0 + c + step].bitcast(FP8X4),
+                    rhs=codes_of(b, m0 + c, m0 + c + step),
                     rhs_scale=x_scales[b][:, m0 + c:m0 + c + step],
-                    start=(b == 0 and k == 0), stop=(b == HB - 1 and k == len(passes) - 1))
+                    start=(b == 0 and j == 0), stop=(b == HB - 1 and j == len(pieces) - 1))
+
+        def finish(i, on_vector):
+            m0, width, row_tiles = units[i]
+            if i >= len(early):
+                score(i, 0)
+            score(i, 1)
+            bank = banks[i % BANKS]
+            stage = staged[i % NT][:, (i // NT) * HALF:(i // NT + 1) * HALF]
+            for k, n in enumerate(row_tiles):
+                cols = slice(k * width, (k + 1) * width)
+                if on_vector:
+                    nc.vector.tensor_scalar(stage[:, cols], bank[:, cols], gain_sb[:, n:n + 1], None, ALU.mult)
+                else:
+                    nc.scalar.activation(stage[:, cols], bank[:, cols], ACT.Copy, scale=gain_sb[:, n:n + 1])
+            rows = out[row_tiles[0] * P:(row_tiles[-1] + 1) * P, m0:m0 + width]
+            nc.sync.dma_start(rows.rearrange("(k p) m -> p k m", p=P), stage.rearrange("p (k m) -> p k m", m=width))
 
         nc.vector.memset(zero_in[:], 0.0)
         nc.scalar.activation(zero[:], zero_in[:], ACT.Tanh)
-        for s in range(2):
-            (nc.gpsimd, nc.vector)[s].memset(scale_win[s][:].bitcast(I32), 0)
+        nc.gpsimd.memset(table_scales[FRONT][:].bitcast(I32), 0)
+        nc.vector.memset(table_scales[BACK][:].bitcast(I32), 0)
         make_identity(nc, identity[:])
-        load_scales(0, range(4), nc.gpsimd)
-        load_scales(1, range(4), nc.gpsimd)
+        load_table_scales(FRONT)
+        load_table_scales(BACK)
         nc.vector.memset(w4s[:].rearrange("p b n -> p (b n)").bitcast(I32), 0)
 
         load_w1(0, 0)
-        load_rowvec(nc.sync, rowgain[0], gf)
+        load_gf(0)
         load_w1(0, 1)
         load_list("offs3", offs3)
         load_w1(0, 2)
-        nc.sync.dma_start(wg_rows[0][:], wg1)
-        load_words(0, 0)
+        nc.sync.dma_start(wg_rows[FRONT][:], wg1)
+        load_words(FRONT, 0)
         load_list("offs", offs)
-        load_words(0, 1)
-        load_rowvec(nc.sync, rowgain[1], gb)
-        load_words(0, 2)
+        load_words(FRONT, 1)
+        load_words(FRONT, 2)
         load_list("offs2", offs2)
         load_page(0)
-        nc.sync.dma_start(wg_rows[1][:], wg2)
+        load_gf(1)
         load_page(1)
+        nc.sync.dma_start(wg_rows[BACK][:], wg2)
+        load_by_row(gb_sb, gb)
         load_page(2)
-        load_words(1, 0)
-        load_words(1, 1)
-        load_words(1, 2)
+        for a in range(KP):
+            load_words(BACK, a)
         load_page(3)
         load_list("offs4", offs4)
         load_page(4)
         load_list("offs5", offs5)
         for a in range(KP):
-            quantize_w1(0, a, 0, 2, nc.vector.tensor_copy)
+            quantize_w1(0, a, 0, VECTOR_CASTS, nc.vector.tensor_copy)
         for a in range(KP):
-            quantize_w1(0, a, 2, PACK)
+            quantize_w1(0, a, VECTOR_CASTS, PACK)
         for a in range(KP):
             load_w1(1, a)
-        load_rowvec(nc.sync, lvl_sb, lvl)
+        load_by_row(lvl_sb, lvl)
         load_page(5)
 
-        make_factors(0)
-        gather_table(0)
-        put(0, 0)
-        put(0, 1)
-        put(0, 2)
-        make_factors(1)
+        deal_wg(FRONT)
+        make_factors(FRONT, 0)
+        gather_table(FRONT)
+        for u in range(PACK):
+            put(FRONT, u)
+        make_factors(FRONT, 1)
+        deal_wg(BACK)
+        for b in range(HB):
+            make_factors(BACK, b)
         load_page(6)
         load_page(7)
         nc.sync.dma_start(w4c[:].bitcast(I32), w4_words.rearrange("b p n -> p b n").bitcast(I32))
-        for q in range(4):
+        for q in range(QUADRANTS):
             nc.sync.dma_start(w4s[32 * q:32 * q + 4, :, :].bitcast(I32),
                               w4_scales[:, 4 * q:4 * q + 4, :].rearrange("b r n -> r b n").bitcast(I32))
         with nc.allow_non_contiguous_dma(reason="one gain value for each partition"):
             nc.sync.dma_start(gain_sb[:], gain.rearrange("(c p) -> p c", p=P))
 
-        gather_table(1)
-        put(0, 3)
-        put(1, 0)
-        put(1, 1)
-        put(1, 2)
-        put(1, 3)
+        gather_table(BACK)
+        for u in range(PACK):
+            put(BACK, u)
         for a in range(KP):
             quantize_w1(1, a)
-            fetch(a)
-
+            fetch(a, fetched(a))
         nc.scalar.mul(neg_lvl[:], lvl_sb[:], -1.0)
-        put(0, 4)
-        put(0, 5)
-        level(0)
-        fetch(3)
-        put(1, 4)
-        put(1, 5)
-        level(1)
-        fetch(4)
-        put(0, 6)
-        level(2)
-        fetch(5)
-        put(1, 6)
-        level(3)
+
+        put(FRONT, 4)
+        put(FRONT, 5)
+        level(0, fetched(0))
+        fetch(3, fetched(3))
+        put(BACK, 4)
+        put(BACK, 5)
+        level(1, fetched(1))
+        fetch(4, fetched(4))
+        put(FRONT, 6)
+        level(2, fetched(2))
+        fetch(5, fetched(5))
+        put(BACK, 6)
+        level(3, fetched(3))
         weave(0, PACK)
-        fetch(6)
-        put(0, 7)
-        quantize_x(0)
-        put(1, 7)
-        level(4)
-        level(5)
-        weave(1, 2)
-        level(6)
+        fetch(6, fetched(6))
+        put(FRONT, LAST)
+        quantize_x(0, 0, HALF)
+        put(BACK, LAST)
+        level(4, fetched(4))
+        level(5, fetched(5))
+        weave(1, PLANAR - PACK)
+        level(6, fetched(6))
 
-        units = [(m0, QUARTER, (n, n + 1)) for m0 in (0, QUARTER) for n in range(0, NT, 2)]
-        units = units + [(HALF, HALF, (n,)) for n in range(NT)]
-        for i in range(BANKS):
-            score(banks[i], 0, units[i])
-        fetch(7, 0, QUARTER, at=0)
-        level(7, 0, QUARTER, at=0)
-        fetch(7, QUARTER, HALF, at=HALF)
-        level(7, QUARTER, HALF, at=HALF)
-        quantize_x(1, 0, QUARTER)
-        fetch(7, HALF, PICK, at=0)
-        quantize_x(1, QUARTER, HALF)
-        level(7, HALF, PICK, at=0)
-
+        x_codes[0, 1] = tile([P, HALF], U32, "xc01", tag="feat%d" % ((len(done_puts) - 1) % FEATS))[:]
+        quarters = tile([P, 2 * QUARTER], F32, "quarters", tag="factor%d%d" % (BACK, LAST))
         staged = [tile([P, PICK], F32, "staged%d" % n, tag="page%d" % n) for n in range(NT)]
-        for i, unit in enumerate(units):
-            if i == LATE:
-                quantize_x(1, HALF, PICK)
-            m0, width, ns = unit
-            bank = banks[i % BANKS]
-            if i >= BANKS:
-                score(bank, 0, unit)
-            score(bank, 1, unit)
-            stage = staged[i % NT][:, (i // NT) * HALF:(i // NT + 1) * HALF]
-            for k, n in enumerate(ns):
-                cols = slice(k * width, (k + 1) * width)
-                if i in ON_VECTOR:
-                    nc.vector.tensor_scalar(stage[:, cols], bank[:, cols], gain_sb[:, n:n + 1], None, ALU.mult)
-                else:
-                    nc.scalar.activation(stage[:, cols], bank[:, cols], ACT.Copy, scale=gain_sb[:, n:n + 1])
-            rows = out[ns[0] * P:(ns[-1] + 1) * P, m0:m0 + width]
-            nc.sync.dma_start(rows.rearrange("(k p) m -> p k m", p=P), stage.rearrange("p (k m) -> p k m", m=width))
+
+        def fetch_quarter(c):
+            slot = quarters[:, (c % 2) * QUARTER:(c % 2 + 1) * QUARTER]
+            fetch(LAST, slot, c * QUARTER, (c + 1) * QUARTER)
+            level(LAST, slot, c * QUARTER, (c + 1) * QUARTER)
+
+        for i in range(len(early)):
+            score(i, 0)
+        fetch_quarter(0)
+        fetch_quarter(1)
+        quantize_x(0, HALF, PICK)
+        quantize_x(1, 0, QUARTER)
+        fetch_quarter(2)
+        quantize_x(1, QUARTER, HALF)
+        fetch_quarter(3)
+        for i in range(len(early)):
+            finish(i, on_vector=(units[i][0] == 0))
+        quantize_x(1, HALF, PICK)
+        for i in range(len(early), len(units)):
+            finish(i, on_vector=(i % 2 == 0))

from contextlib import ExitStack

import concourse.mybir as mybir
from concourse.masks import make_identity

K, T, S, H, T2, PICK, N = 1536, 2048, 512, 1024, 2048, 1024, 768
FLOPS = 2 * (2 * K * H * S + H * N * PICK)

F32 = mybir.dt.float32
BF16 = mybir.dt.bfloat16
I32 = mybir.dt.int32
U32 = mybir.dt.uint32
U16 = mybir.dt.uint16
U8 = mybir.dt.uint8
FP8X4 = mybir.dt.float8_e4m3fn_x4
FP4X4 = mybir.dt.float4_e2m1fn_x4
ACT = mybir.ActivationFunctionType
ALU = mybir.AluOpType

P = 128
PACK = 4
PASS = P * PACK
KP = K // PASS
HB = H // PASS
TILES = HB * PACK
LAST = TILES - 1
NT = N // P
BANKS = 8
HALF = 512
QUARTER = 256
QUADRANTS = 4
FEATS = 6
PLANAR = 6
VECTOR_CASTS = 2
FRONT, BACK = 0, 1


def tile_list_banknote_fitness_archive_kernel(
    tc, tab_words, tab_scales, tab2_words, tab2_scales, offs, offs2, offs3, offs4, offs5,
    w1, gf, gb, wg1, wg2, page0, lvl, w4_words, w4_scales, gain, out,
):
    nc = tc.nc
    with ExitStack() as ctx:
        sb = ctx.enter_context(tc.tile_pool(name="sb", bufs=1))
        ps = ctx.enter_context(tc.psum_pool(name="ps", bufs=1))

        def tile(shape, dtype, name, tag=None):
            return sb.tile(shape, dtype, name=name, tag=tag or name, align_bytes=64)

        banks = [ps.tile([P, HALF], F32, name="bank%d" % i, tag="bank%d" % i) for i in range(BANKS)]
        staging = [tile([P, PACK * PASS], F32, "staging%d" % a) for a in range(KP)]
        grouped = [tile([P, PACK * PASS], BF16, "grouped%d" % a) for a in range(KP)]
        w1_codes = [[tile([P, PASS], U32, "w1c%d%d" % (b, a)) for a in range(KP)] for b in range(HB)]
        w1_scales = [[tile([P, PASS], U8, "w1s%d%d" % (b, a)) for a in range(KP)] for b in range(HB)]
        words = [[tile([P, T], U32, "words%d%d" % (s, a)) for a in range(KP)] for s in (FRONT, BACK)]
        table_scales = [tile([P, T], U8, "table_scales%d" % s) for s in (FRONT, BACK)]
        v_codes = [[tile([P, S], U32, "vc%d%d" % (s, a)) for a in range(KP)] for s in (FRONT, BACK)]
        spread = [tile([P, PACK * S], F32, "spread%d" % s, tag="page%d" % (LAST - s)) for s in (FRONT, BACK)]
        pages = [tile([P, T2], F32, "page%d" % u) for u in range(TILES)]
        wg_rows = [tile([P, S], F32, "wg_rows%d" % s) for s in (FRONT, BACK)]
        factor = [[tile([P, S], F32, "factor%d%d" % (s, u)) for u in range(TILES)] for s in (FRONT, BACK)]
        v_scales = [tile([P, S], U8, "vs%d" % s) for s in (FRONT, BACK)]
        identity = tile([P, P], F32, "identity")
        feat = [tile([P, S], F32, "feat%d" % i) for i in range(FEATS)]
        w4c = tile([P, HB, 2 * N], U8, "w4c")
        w4s = tile([P, HB, N], U8, "w4s")
        gf_sb = [tile([P, PACK], F32, "gf_sb%d" % b) for b in range(HB)]
        gb_sb = tile([P, HB, PACK], F32, "gb_sb")
        row_gain = [[gf_sb[b][:] for b in range(HB)], [gb_sb[:, b] for b in range(HB)]]
        lvl_sb = tile([P, HB, PACK], F32, "lvl_sb")
        neg_lvl = tile([P, HB, PACK], F32, "neg_lvl")
        gain_sb = tile([P, NT], F32, "gain_sb")
        zero_in = tile([P, 1], F32, "zero_in")
        zero = tile([P, 1], F32, "zero")
        x_codes = {(0, 0): tile([P, HALF], U32, "xc00", tag="words10")[:]}
        last_codes = tile([P, PICK], U32, "xc1", tag="words11")
        x_codes[1, 0], x_codes[1, 1] = last_codes[:, 0:HALF], last_codes[:, HALF:PICK]
        x_scales = [tile([P, PICK], U8, "xs%d" % b) for b in range(HB)]
        planes = tile([P, PACK * PICK], BF16, "planes", tag="words02")
        woven = [tile([P, PICK * PACK], BF16, "woven%d" % b, tag="words0%d" % b) for b in range(HB)]
        lists = {}
        done_puts = []

        def load_list(name, src):
            lists[name] = tile([P, src.shape[1]], U16, "list_" + name)
            nc.sync.dma_start(lists[name][:], src)

        def load_w1(b, a):
            nc.sync.dma_start(
                staging[a][:].rearrange("p (j c) -> p j c", j=PACK),
                w1[a * PASS:(a + 1) * PASS, b * PASS:(b + 1) * PASS].rearrange("(p j) c -> p j c", j=PACK))

        def load_words(s, a):
            src = (tab_words, tab2_words)[s]
            nc.sync.dma_start(words[s][a][:].bitcast(I32), src[a].rearrange("p t i -> p (t i)").bitcast(I32))

        def load_table_scales(s):
            src = (tab_scales, tab2_scales)[s]
            for q in range(QUADRANTS):
                nc.gpsimd.dma_start(table_scales[s][32 * q:32 * q + 4 * KP, :].bitcast(I32),
                                    src[:, 4 * q:4 * q + 4, :].bitcast(I32))

        def load_page(u):
            b, t = divmod(u, PACK)
            nc.sync.dma_start(pages[u][:], page0.rearrange("(b p t) c -> b t p c", b=HB, t=PACK)[b, t])

        def load_gf(b):
            nc.sync.dma_start(gf_sb[b][:], gf[b * PASS:(b + 1) * PASS].rearrange("(p t) -> p t", t=PACK))

        def load_by_row(dst, src):
            nc.sync.dma_start(dst[:], src.rearrange("(b p t) -> p b t", b=HB, t=PACK))

        turned = banks[7]
        dealt = [banks[6], banks[5], banks[4], turned]

        def deal_wg(s):
            for c in range(S // P):
                cols = slice(c * P, (c + 1) * P)
                nc.tensor.transpose(turned[:, cols], wg_rows[s][:, cols], identity[:])
            for t in range(PACK):
                picked = turned[:].rearrange("j (c q t) -> j t c q", c=S // P, t=PACK)[:, t]
                nc.scalar.copy(
                    spread[s][:, t * S:(t + 1) * S].rearrange("j (c r q) -> j c r q", c=S // P, r=PACK),
                    picked.unsqueeze(2).to_broadcast([P, S // P, PACK, P // PACK]))
                for c in range(S // P):
                    nc.tensor.transpose(dealt[t][:, c * P:(c + 1) * P],
                                        spread[s][:, t * S + c * P:t * S + (c + 1) * P], identity[:])

        def make_factors(s, b):
            for t in range(PACK):
                nc.scalar.activation(factor[s][PACK * b + t][:], dealt[t][:], ACT.Copy,
                                     scale=row_gain[s][b][:, t:t + 1])

        def quantize_w1(b, a, t0=0, t1=PACK, cast=nc.scalar.copy):
            cast(grouped[a][:].rearrange("p (t m j) -> p t m j", t=PACK, j=PACK)[:, t0:t1],
                 staging[a][:].rearrange("p (j m t) -> p t m j", j=PACK, t=PACK)[:, t0:t1])
            cols = slice(t0 * P, t1 * P)
            nc.vector.quantize_mx(out=w1_codes[b][a][:, cols].bitcast(FP8X4), scales=w1_scales[b][a][:, cols],
                                  in_=grouped[a][:, t0 * PASS:t1 * PASS])

        def gather_table(s):
            offsets = lists[("offs", "offs2")[s]]
            nc.vector.tensor_copy(v_scales[s][:], table_scales[s][:].indirect(offsets[:]))
            for a in range(KP):
                nc.vector.tensor_copy(v_codes[s][a][:], words[s][a][:].indirect(offsets[:]))

        def put(s, u):
            count = len(done_puts)
            done_puts.append((s, u))
            b, t = divmod(u, PACK)
            bank = banks[t if b == 0 else count % BANKS]
            cols = slice(t * P, (t + 1) * P)
            for a in range(KP):
                nc.tensor.matmul_mx(
                    out=bank[:], lhsT=w1_codes[b][a][:, cols].bitcast(FP8X4), lhsT_scale=w1_scales[b][a][:, cols],
                    rhs=v_codes[s][a][:].bitcast(FP8X4), rhs_scale=v_scales[s][4 * a:P, :],
                    start=(a == 0), stop=(a == KP - 1))
            features = feat[count % FEATS]
            nc.scalar.activation(features[:], bank[:], (ACT.Tanh, ACT.Square)[s], bias=zero[:])
            offsets = lists[("offs3", "offs4")[s]]
            nc.vector.tensor_tensor(pages[u][:].indirect(offsets[:]), features[:], factor[s][u][:], ALU.mult)

        def fetch(u, dst, m0=0, m1=PICK):
            nc.vector.tensor_copy(dst, pages[u][:].indirect(lists["offs5"][:, m0 // 16:m1 // 16]))

        def level(u, src, m0=0, m1=PICK):
            b, t = divmod(u, PACK)
            if u < PLANAR:
                dst = planes[:, t * PICK:(t + 1) * PICK]
            else:
                dst = woven[b][:].rearrange("p (m t) -> p m t", t=PACK)[:, m0:m1, t]
            nc.scalar.activation(dst, src, ACT.Identity, bias=neg_lvl[:, b, t:t + 1])

        def fetched(u):
            return staging[u % KP][:, 0:PICK]

        def weave(b, count):
            nc.scalar.copy(woven[b][:].rearrange("p (m t) -> p m t", t=PACK)[:, :, 0:count],
                           planes[:].rearrange("p (t m) -> p m t", t=PACK)[:, :, 0:count])

        def codes_of(b, m0, m1):
            half, start = divmod(m0, HALF)
            return x_codes[b, half][:, start:start + m1 - m0].bitcast(FP8X4)

        def quantize_x(b, m0, m1):
            nc.vector.quantize_mx(out=codes_of(b, m0, m1), scales=x_scales[b][:, m0:m1],
                                  in_=woven[b][:, PACK * m0:PACK * m1])

        early = [(m0, QUARTER, (n, n + 1)) for m0 in (0, QUARTER) for n in range(0, NT, 2)]
        units = early + [(HALF, HALF, (n,)) for n in range(NT)]

        def score(i, b):
            m0, width, row_tiles = units[i]
            step = HALF if width == HALF else P
            pieces = [(k, n, c) for k, n in enumerate(row_tiles) for c in range(0, width, step)]
            for j, (k, n, c) in enumerate(pieces):
                nc.tensor.matmul_mx(
                    out=banks[i % BANKS][:, k * width + c:k * width + c + step],
                    lhsT=w4c[:, b, 2 * P * n:2 * P * (n + 1)].bitcast(FP4X4),
                    lhsT_scale=w4s[:, b, P * n:P * (n + 1)],
                    rhs=codes_of(b, m0 + c, m0 + c + step),
                    rhs_scale=x_scales[b][:, m0 + c:m0 + c + step],
                    start=(b == 0 and j == 0), stop=(b == HB - 1 and j == len(pieces) - 1))

        def finish(i, on_vector):
            m0, width, row_tiles = units[i]
            if i >= len(early):
                score(i, 0)
            score(i, 1)
            bank = banks[i % BANKS]
            stage = staged[i % NT][:, (i // NT) * HALF:(i // NT + 1) * HALF]
            for k, n in enumerate(row_tiles):
                cols = slice(k * width, (k + 1) * width)
                if on_vector:
                    nc.vector.tensor_scalar(stage[:, cols], bank[:, cols], gain_sb[:, n:n + 1], None, ALU.mult)
                else:
                    nc.scalar.activation(stage[:, cols], bank[:, cols], ACT.Copy, scale=gain_sb[:, n:n + 1])
            rows = out[row_tiles[0] * P:(row_tiles[-1] + 1) * P, m0:m0 + width]
            nc.sync.dma_start(rows.rearrange("(k p) m -> p k m", p=P), stage.rearrange("p (k m) -> p k m", m=width))

        nc.vector.memset(zero_in[:], 0.0)
        nc.scalar.activation(zero[:], zero_in[:], ACT.Tanh)
        nc.gpsimd.memset(table_scales[FRONT][:].bitcast(I32), 0)
        nc.vector.memset(table_scales[BACK][:].bitcast(I32), 0)
        make_identity(nc, identity[:])
        load_table_scales(FRONT)
        load_table_scales(BACK)
        nc.vector.memset(w4s[:].rearrange("p b n -> p (b n)").bitcast(I32), 0)

        load_w1(0, 0)
        load_gf(0)
        load_w1(0, 1)
        load_list("offs3", offs3)
        load_w1(0, 2)
        nc.sync.dma_start(wg_rows[FRONT][:], wg1)
        load_words(FRONT, 0)
        load_list("offs", offs)
        load_words(FRONT, 1)
        load_words(FRONT, 2)
        load_list("offs2", offs2)
        load_page(0)
        load_gf(1)
        load_page(1)
        nc.sync.dma_start(wg_rows[BACK][:], wg2)
        load_by_row(gb_sb, gb)
        load_page(2)
        for a in range(KP):
            load_words(BACK, a)
        load_page(3)
        load_list("offs4", offs4)
        load_page(4)
        load_list("offs5", offs5)
        for a in range(KP):
            quantize_w1(0, a, 0, VECTOR_CASTS, nc.vector.tensor_copy)
        for a in range(KP):
            quantize_w1(0, a, VECTOR_CASTS, PACK)
        for a in range(KP):
            load_w1(1, a)
        load_by_row(lvl_sb, lvl)
        load_page(5)

        deal_wg(FRONT)
        make_factors(FRONT, 0)
        gather_table(FRONT)
        for u in range(PACK):
            put(FRONT, u)
        make_factors(FRONT, 1)
        deal_wg(BACK)
        for b in range(HB):
            make_factors(BACK, b)
        load_page(6)
        load_page(7)
        nc.sync.dma_start(w4c[:].bitcast(I32), w4_words.rearrange("b p n -> p b n").bitcast(I32))
        for q in range(QUADRANTS):
            nc.sync.dma_start(w4s[32 * q:32 * q + 4, :, :].bitcast(I32),
                              w4_scales[:, 4 * q:4 * q + 4, :].rearrange("b r n -> r b n").bitcast(I32))
        with nc.allow_non_contiguous_dma(reason="one gain value for each partition"):
            nc.sync.dma_start(gain_sb[:], gain.rearrange("(c p) -> p c", p=P))

        gather_table(BACK)
        for u in range(PACK):
            put(BACK, u)
        for a in range(KP):
            quantize_w1(1, a)
            fetch(a, fetched(a))
        nc.scalar.mul(neg_lvl[:], lvl_sb[:], -1.0)

        put(FRONT, 4)
        put(FRONT, 5)
        level(0, fetched(0))
        fetch(3, fetched(3))
        put(BACK, 4)
        put(BACK, 5)
        level(1, fetched(1))
        fetch(4, fetched(4))
        put(FRONT, 6)
        level(2, fetched(2))
        fetch(5, fetched(5))
        put(BACK, 6)
        level(3, fetched(3))
        weave(0, PACK)
        fetch(6, fetched(6))
        put(FRONT, LAST)
        quantize_x(0, 0, HALF)
        put(BACK, LAST)
        level(4, fetched(4))
        level(5, fetched(5))
        weave(1, PLANAR - PACK)
        level(6, fetched(6))

        x_codes[0, 1] = tile([P, HALF], U32, "xc01", tag="feat%d" % ((len(done_puts) - 1) % FEATS))[:]
        quarters = tile([P, 2 * QUARTER], F32, "quarters", tag="factor%d%d" % (BACK, LAST))
        staged = [tile([P, PICK], F32, "staged%d" % n, tag="page%d" % n) for n in range(NT)]

        def fetch_quarter(c):
            slot = quarters[:, (c % 2) * QUARTER:(c % 2 + 1) * QUARTER]
            fetch(LAST, slot, c * QUARTER, (c + 1) * QUARTER)
            level(LAST, slot, c * QUARTER, (c + 1) * QUARTER)

        for i in range(len(early)):
            score(i, 0)
        fetch_quarter(0)
        fetch_quarter(1)
        quantize_x(0, HALF, PICK)
        quantize_x(1, 0, QUARTER)
        fetch_quarter(2)
        quantize_x(1, QUARTER, HALF)
        fetch_quarter(3)
        for i in range(len(early)):
            finish(i, on_vector=(units[i][0] == 0))
        quantize_x(1, HALF, PICK)
        for i in range(len(early), len(units)):
            finish(i, on_vector=(i % 2 == 0))
